import numpy as np
import ml_dtypes


def mxq(x, axis, fmt="e4m3"):
    dtype, down = {"e4m3": (ml_dtypes.float8_e4m3fn, 7), "e5m2": (ml_dtypes.float8_e5m2, 14)}[fmt]
    v = np.moveaxis(np.asarray(x, np.float32).astype(ml_dtypes.bfloat16).astype(np.float64), axis, -1)
    blocks = v.reshape(v.shape[:-1] + (-1, 32))
    amax = np.abs(blocks).max(-1, keepdims=True)
    byte = np.maximum(np.where(amax > 0, np.frexp(amax)[1] - 1 + 127, 0) - down, 1)
    scale = np.exp2(byte - 127.0)
    codes = (blocks / scale).astype(np.float32).astype(dtype).astype(np.float64)
    return np.moveaxis((codes * scale).reshape(v.shape), -1, axis)


WIDE = False


def mx_kscale(k):
    if not WIDE:
        return np.ones(k)
    levels = np.array([10, -10, 5, -5, 0])
    if k % 512:
        return np.exp2(np.random.permutation(np.resize(levels, k // 32))).repeat(32)
    a = np.empty((k // 512, 16))
    for p in range(k // 512):
        a[p, :8] = np.random.permutation(np.resize(levels, 8))
        for g in range(8):
            far = levels[np.abs(levels - a[p, g]) >= 10]
            a[p, g + 8] = far[np.random.randint(len(far))]
    return np.exp2(a.ravel()).repeat(32)


def f64(x):
    return np.asarray(x).astype(np.float64)


def striped(idx):
    return np.tile(idx.reshape(-1, 16).T, (8, 1)).astype(np.uint16)


def unstriped(offs):
    return offs[:16].T.reshape(-1).astype(np.int64)


def striped8(idx):
    return np.concatenate([x.reshape(-1, 16).T for x in idx]).astype(np.uint16)


def runs(offs, k):
    lists = np.stack([offs[16 * r : 16 * r + 16].T.reshape(-1) for r in range(8)]).astype(np.int64)
    return lists[np.arange(k) % 512 // 64]


def pack_weight(w):
    k, n = w.shape
    w = f64(np.asarray(w, np.float32).astype(ml_dtypes.bfloat16)).reshape(k // 32, 32, n)
    amax = np.abs(w).max(1)
    byte = np.clip(np.where(amax > 0, np.frexp(amax)[1] - 1 + 127 - 7, 1), 1, 254)
    scaled = (w * np.exp2(127.0 - byte)[:, None, :]).reshape(k, n).astype(np.float32)
    words = np.ascontiguousarray(scaled.reshape(k // 512, 128, 4, n).transpose(0, 1, 3, 2)).astype(ml_dtypes.float8_e4m3fn).view(np.uint8)
    return words, np.ascontiguousarray(byte.astype(np.uint8).reshape(k // 512, 16, n))


def unpack_weight(words, scales):
    g, p, n, _ = words.shape
    vals = np.ascontiguousarray(words).view(ml_dtypes.float8_e4m3fn).astype(np.float64) * np.repeat(np.exp2(scales.astype(np.float64) - 127.0), 8, axis=1)[..., None]
    return vals.transpose(0, 1, 3, 2).reshape(g * 512, n)

def planes(y):
    n, m = y.shape
    v = y.astype(np.float32).astype(ml_dtypes.bfloat16).astype(np.float64).reshape(n // 32, 32, m)
    top = np.abs(v).max(1)
    byte = np.clip(np.where(top > 0, np.frexp(top)[1] - 1 + 127 - 7, 1), 1, 254)
    codes = (v * np.exp2(127.0 - byte)[:, None, :]).reshape(n, m).astype(np.float32).astype(ml_dtypes.float8_e4m3fn).view(np.uint8)
    words = codes.reshape(n // 512, 128, 4, m).transpose(0, 1, 3, 2)
    return np.ascontiguousarray(words), np.ascontiguousarray(byte.astype(np.uint8).reshape(n // 512, 16, m))


K, T, S, N, H = 512, 2048, 512, 512, 512


def setup_inputs():
    n = np.random.standard_normal
    s = mx_kscale(K)[:, None]
    u = mx_kscale(H)
    packed_xT = pack_weight(n((K, T)) * s)
    packed_w1 = pack_weight(n((K, H)) / np.sqrt(K) / s)
    packed_w2 = pack_weight(n((H, N)) / np.sqrt(H) / u[:, None])
    return {
        "x_words": packed_xT[0],
        "x_scales": packed_xT[1],
        "w1_words": packed_w1[0],
        "w1_scales": packed_w1[1],
        "gn": (np.random.uniform(0.5, 1.5, (H, 1)) * u[:, None]).astype(np.float32),
        "w2_words": packed_w2[0],
        "w2_scales": packed_w2[1],
        "offs": striped(np.random.permutation(T)[:S]),
        "p1": striped8(np.stack([np.random.permutation(S) for _ in range(8)])),
        "p2": striped8(np.stack([np.random.permutation(S) for _ in range(8)])),
    }


def reference(x_words, x_scales, w1_words, w1_scales, gn, w2_words, w2_scales, offs, p1, p2):
    xq = unpack_weight(x_words, x_scales)[:, unstriped(offs)]
    y = unpack_weight(w1_words, w1_scales).T @ xq
    a = y[np.arange(H)[:, None], runs(p1, H)]
    b = y[np.arange(H)[:, None], runs(p2, H)]
    mu = 0.3125 * (y + a + b)
    vr = (y - mu) ** 2 + (a - mu) ** 2 + (b - mu) ** 2
    z = f64(gn) * ((y - mu) / np.sqrt(0.25 * vr + 0.1))
    out_0 = unpack_weight(w2_words, w2_scales).T @ mxq(z, 0, "e4m3")
    return (out_0,) + planes(out_0)

@@ -1,0 +1,218 @@
+from contextlib import ExitStack
+import math
+
+import concourse.mybir as mybir
+from concourse.masks import make_identity
+
+K, T, S, N, H = 512, 2048, 512, 512, 512
+FLOPS = 2 * K * H * S + 2 * H * N * S
+
+F32 = mybir.dt.float32
+BF16 = mybir.dt.bfloat16
+I32 = mybir.dt.int32
+U32 = mybir.dt.uint32
+U16 = mybir.dt.uint16
+U8 = mybir.dt.uint8
+FP8X4 = mybir.dt.float8_e4m3fn_x4
+ALU = mybir.AluOpType
+ACT = mybir.ActivationFunctionType
+
+P = 128
+PACK = 4
+BLOCK = 128
+CHUNKS = [256, 128, 128]
+
+C = 0.3125
+KAPPA = 2 * C - 3 * C * C
+BETA = 0.5 - KAPPA
+ETA = KAPPA / BETA
+PHI = 1.0 - KAPPA - KAPPA * KAPPA / BETA
+NU = (1.0 - C) / C
+OUTER = 0.25 / (C * C)
+FLOOR = 0.1 / (C * C)
+
+
+def load_scale_rows(queues, tile, rows):
+    for q in range(4):
+        queues[q].dma_start(out=tile[32 * q : 32 * q + 4, :].bitcast(I32), in_=rows[4 * q : 4 * q + 4, :].bitcast(I32))
+
+
+def words_of(ap):
+    return ap[0].rearrange("p n t -> p (n t)").bitcast(I32)
+
+
+def tile_picked_zscore3_none_po_kernel(
+    tc, x_words, x_scales, w1_words, w1_scales, gn, w2_words, w2_scales, offs, p1, p2, out_0, out_1, out_2
+):
+    nc = tc.nc
+    with ExitStack() as ctx:
+        keep = ctx.enter_context(tc.tile_pool(name="keep", bufs=1))
+        ring = ctx.enter_context(tc.tile_pool(name="ring", bufs=2))
+        psum = ctx.enter_context(tc.psum_pool(name="psum", bufs=8))
+
+        offs_t = keep.tile([P, S // 16], U16, name="offs_t")
+        p1_t = keep.tile([P, S // 16], U16, name="p1_t")
+        p2_t = keep.tile([P, S // 16], U16, name="p2_t")
+        x_w = keep.tile([P, T], I32, name="x_w", align_bytes=64)
+        x_s = keep.tile([P, T], U8, name="x_s", align_bytes=64)
+        w_w = keep.tile([P, H], I32, name="w_w", align_bytes=64)
+        w_s = keep.tile([P, H], U8, name="w_s", align_bytes=64)
+        gain = keep.tile([P, PACK], F32, name="gain")
+
+        ident = keep.tile([P, P], F32, name="ident")
+        gain_neg = keep.tile([P, PACK], F32, name="gain_neg")
+        gain_nu = keep.tile([P, PACK], F32, name="gain_nu")
+
+        nc.vector.memset(w_s[:].bitcast(I32), 0)
+        nc.vector.memset(x_s[:].bitcast(I32), 0)
+        nc.vector.memset(ident[:], 0.0)
+
+        nc.sync.dma_start(offs_t[:], offs)
+        nc.scalar.dma_start(out=gain[:], in_=gn.rearrange("(p t) o -> p (t o)", t=PACK))
+        nc.sync.dma_start(p1_t[:], p1)
+        nc.sync.dma_start(p2_t[:], p2)
+        nc.sync.dma_start(out=x_w[:], in_=words_of(x_words))
+        nc.sync.dma_start(out=w_w[:], in_=words_of(w1_words))
+        load_scale_rows([nc.scalar] * 4, x_s, x_scales[0])
+        load_scale_rows([nc.gpsimd, nc.gpsimd, nc.sync, nc.sync], w_s, w1_scales[0])
+        make_identity(nc, ident[:], nomemset=True)
+
+        xg_w = keep.tile([P, S], I32, name="xg_w", align_bytes=64)
+        xg_s = keep.tile([P, S], U8, name="xg_s", align_bytes=64)
+        w1d_w = keep.tile([P, H], I32, name="w1d_w", align_bytes=64)
+        w1d_s = keep.tile([P, H], U8, name="w1d_s", align_bytes=64)
+        w2d_w = keep.tile([P, N], I32, name="w2d_w", align_bytes=64)
+        w2d_s = keep.tile([P, N], U8, name="w2d_s", align_bytes=64)
+
+        def deal(dst, src):
+            nc.vector.tensor_copy(
+                out=dst[:].rearrange("p (t m) -> p t m", t=PACK), in_=src[:].rearrange("p (m t) -> p t m", t=PACK)
+            )
+
+        nc.vector.tensor_copy(xg_s[:], x_s[:].indirect(offs_t[:]))
+        deal(w1d_s, w_s)
+        halves = [slice(0, S // 2), slice(S // 2, S)]
+        w1_view = w_w[:].rearrange("p (m t) -> p t m", t=PACK)
+        nc.vector.tensor_copy(xg_w[:, halves[0]].bitcast(U32), x_w[:].bitcast(U32).indirect(offs_t[:, 0:16]))
+        nc.vector.tensor_copy(out=w1d_w[:, 0:P], in_=w1_view[:, 0, :])
+        nc.vector.tensor_copy(xg_w[:, halves[1]].bitcast(U32), x_w[:].bitcast(U32).indirect(offs_t[:, 16:32]))
+        for t in range(1, PACK):
+            nc.vector.tensor_copy(out=w1d_w[:, t * P : (t + 1) * P], in_=w1_view[:, t, :])
+        nc.vector.tensor_scalar(out=gain_nu[:], in0=gain[:], scalar1=NU, scalar2=None, op0=ALU.mult)
+        nc.vector.tensor_scalar(out=gain_neg[:], in0=gain[:], scalar1=-1.0, scalar2=None, op0=ALU.mult)
+
+        y = [keep.tile([P, S], F32, name="y%d" % t) for t in range(PACK)]
+        for t in range(PACK):
+            cols = slice(t * P, (t + 1) * P)
+            for half in halves:
+                bank = psum.tile([P, S // 2], F32, name="bank")
+                nc.tensor.matmul_mx(
+                    out=bank[:], lhsT=w1d_w[:, cols].bitcast(FP8X4), lhsT_scale=w1d_s[:, cols],
+                    rhs=xg_w[:, half].bitcast(FP8X4), rhs_scale=xg_s[:, half], start=True, stop=True,
+                )
+                nc.scalar.copy(out=y[t][:, half], in_=bank[:])
+        nc.sync.dma_start(out=w_w[:], in_=words_of(w2_words))
+        load_scale_rows([nc.sync] * 4, w_s, w2_scales[0])
+        deal(w2d_w, w_w)
+        deal(w2d_s, w_s)
+
+        o_w = keep.tile([P, S], I32, name="o_w", align_bytes=64)
+        o_s = keep.tile([P, S], U8, name="o_s", align_bytes=64)
+        out_rows = out_0.rearrange("(p t) j -> p t j", t=PACK)
+        out_words = words_of(out_1)
+
+        state = {}
+
+        def fetch(j0, cw):
+            lst = slice(j0 // 16, (j0 + cw) // 16)
+            cols = slice(j0, j0 + cw)
+            a = ring.tile([P, PACK, cw], F32, name="a")
+            ab = ring.tile([P, PACK, cw], F32, name="ab")
+            y_sq = ring.tile([P, PACK, cw], F32, name="y_sq")
+            y_g = ring.tile([P, PACK, cw], F32, name="y_g")
+            for t in range(PACK):
+                nc.scalar.activation(out=y_g[:, t, :], in_=y[t][:, cols], func=ACT.Copy, scale=gain_nu[:, t : t + 1])
+            for t in range(PACK):
+                nc.scalar.activation(out=y_sq[:, t, :], in_=y[t][:, cols], func=ACT.Square, scale=math.sqrt(OUTER * PHI))
+            for pair in ((0, 1), (2, 3)):
+                for t in pair:
+                    nc.vector.tensor_copy(a[:, t, :], y[t][:].indirect(p1_t[:, lst]))
+                for t in pair:
+                    nc.vector.tensor_tensor(ab[:, t, :], y[t][:].indirect(p2_t[:, lst]), a[:, t, :], ALU.add)
+            d = ring.tile([P, PACK, cw], F32, name="d")
+            w = ring.tile([P, PACK, cw], F32, name="w")
+            n = ring.tile([P, PACK, cw], F32, name="n")
+            for t in range(PACK):
+                nc.vector.scalar_tensor_tensor(out=w[:, t, :], in0=y[t][:, cols], scalar=ETA, in1=ab[:, t, :], op0=ALU.mult, op1=ALU.subtract)
+            nc.vector.scalar_tensor_tensor(out=d[:], in0=a[:], scalar=2.0, in1=ab[:], op0=ALU.mult, op1=ALU.subtract)
+            for t in range(PACK):
+                nc.vector.scalar_tensor_tensor(out=n[:, t, :], in0=ab[:, t, :], scalar=gain_neg[:, t : t + 1], in1=y_g[:, t, :], op0=ALU.mult, op1=ALU.add)
+            d_sq = ring.tile([P, PACK, cw], F32, name="d_sq")
+            w_sq = ring.tile([P, PACK, cw], F32, name="w_sq")
+            nc.scalar.activation(out=w_sq[:], in_=w[:], func=ACT.Square, scale=math.sqrt(OUTER * BETA))
+            nc.scalar.activation(out=d_sq[:], in_=d[:], func=ACT.Square, scale=math.sqrt(OUTER * 0.5))
+            state[j0] = (n, [y_sq, w_sq, d_sq])
+
+        def spread(j0, cw):
+            n, squares = state[j0]
+            roots = []
+            for b in range(0, cw, BLOCK):
+                var = psum.tile([P, PACK, P], F32, name="bank")
+                for t in range(PACK):
+                    for i, sq in enumerate(squares):
+                        nc.tensor.matmul(var[:, t, :], lhsT=sq[:, t, b : b + BLOCK], rhs=ident[:], is_transpose=True, start=(i == 0), stop=(i == 2))
+                r_turned = ring.tile([P, PACK, P], F32, name="r_turned")
+                nc.scalar.activation(out=r_turned[:], in_=var[:], func=ACT.Abs_reciprocal_sqrt, bias=FLOOR)
+                r = psum.tile([P, PACK, BLOCK], F32, name="bank")
+                for t in range(PACK):
+                    nc.tensor.transpose(r[:, t, :], r_turned[:, t, :], ident[:])
+                roots.append(r)
+            state[j0] = (n, roots)
+
+        def score(j0, cw):
+            n, roots = state[j0]
+            zi = ring.tile([P, cw, PACK], BF16, name="zi", align_bytes=64)
+            for i, r in enumerate(roots):
+                cols = slice(i * BLOCK, (i + 1) * BLOCK)
+                nc.vector.tensor_tensor(zi[:, cols, :], n[:, :, cols].rearrange("p t j -> p j t"), r[:].rearrange("p t j -> p j t"), ALU.mult)
+            state[j0] = zi
+
+        def second(j0, cw):
+            zi = state[j0]
+            z_w = ring.tile([P, cw], U32, name="z_w", align_bytes=64)
+            z_s = ring.tile([P, cw], U8, name="z_s", align_bytes=64)
+            nc.vector.quantize_mx(out=z_w[:].bitcast(FP8X4), scales=z_s[:], in_=zi[:].rearrange("p j t -> p (j t)"))
+            outs = []
+            for b in range(0, cw, BLOCK):
+                acc = psum.tile([P, PACK, BLOCK], F32, name="bank")
+                for t in range(PACK):
+                    cols = slice(t * P, (t + 1) * P)
+                    nc.tensor.matmul_mx(
+                        out=acc[:, t, :], lhsT=w2d_w[:, cols].bitcast(FP8X4), lhsT_scale=w2d_s[:, cols],
+                        rhs=z_w[:, b : b + BLOCK].bitcast(FP8X4), rhs_scale=z_s[:, b : b + BLOCK], start=True, stop=True,
+                    )
+                o32 = keep.tile([P, PACK, BLOCK], F32, name="o32_%d" % (j0 + b))
+                o16 = keep.tile([P, BLOCK, PACK], BF16, name="o16_%d" % (j0 + b), align_bytes=64)
+                nc.scalar.copy(out=o16[:], in_=acc[:].rearrange("p t j -> p j t"))
+                nc.scalar.copy(out=o32[:], in_=acc[:])
+                nc.sync.dma_start(out=out_rows[:, :, j0 + b : j0 + b + BLOCK], in_=o32[:])
+                outs.append((j0 + b, o16))
+            state[j0] = outs
+
+        def planes(j0, cw):
+            for j, o16 in state[j0]:
+                cols = slice(j, j + BLOCK)
+                nc.vector.quantize_mx(out=o_w[:, cols].bitcast(FP8X4), scales=o_s[:, cols], in_=o16[:].rearrange("p j t -> p (j t)"))
+            nc.sync.dma_start(out=out_words[:, j0 : j0 + cw], in_=o_w[:, j0 : j0 + cw])
+
+        starts = [sum(CHUNKS[:i]) for i in range(len(CHUNKS))]
+        stages = [fetch, spread, score, second, planes]
+        for step in range(len(CHUNKS) + len(stages) - 1):
+            for s in reversed(range(len(stages))):
+                i = step - s
+                if 0 <= i < len(CHUNKS):
+                    stages[s](starts[i], CHUNKS[i])
+
+        for q in range(4):
+            queue = nc.scalar if q % 2 else nc.sync
+            queue.dma_start(out=out_2[0][4 * q : 4 * q + 4, :].bitcast(I32), in_=o_s[32 * q : 32 * q + 4, :].bitcast(I32))

@@ -2,7 +2,6 @@ from contextlib import ExitStack
 import math
 
 import concourse.mybir as mybir
-from concourse.masks import make_identity
 
 K, T, S, N, H = 512, 2048, 512, 512, 512
 FLOPS = 2 * K * H * S + 2 * H * N * S
@@ -20,7 +19,8 @@ ACT = mybir.ActivationFunctionType
 P = 128
 PACK = 4
 BLOCK = 128
-CHUNKS = [256, 128, 128]
+CHUNKS = [256,128,128]
+PE_CHUNKS = []
 
 C = 0.3125
 KAPPA = 2 * C - 3 * C * C
@@ -47,7 +47,7 @@ def tile_picked_zscore3_none_po_kernel(
     nc = tc.nc
     with ExitStack() as ctx:
         keep = ctx.enter_context(tc.tile_pool(name="keep", bufs=1))
-        ring = ctx.enter_context(tc.tile_pool(name="ring", bufs=2))
+        ring = ctx.enter_context(tc.tile_pool(name="ring", bufs=3))
         psum = ctx.enter_context(tc.psum_pool(name="psum", bufs=8))
 
         offs_t = keep.tile([P, S // 16], U16, name="offs_t")
@@ -59,23 +59,17 @@ def tile_picked_zscore3_none_po_kernel(
         w_s = keep.tile([P, H], U8, name="w_s", align_bytes=64)
         gain = keep.tile([P, PACK], F32, name="gain")
 
-        ident = keep.tile([P, P], F32, name="ident")
-        gain_neg = keep.tile([P, PACK], F32, name="gain_neg")
-        gain_nu = keep.tile([P, PACK], F32, name="gain_nu")
-
-        nc.vector.memset(w_s[:].bitcast(I32), 0)
         nc.vector.memset(x_s[:].bitcast(I32), 0)
-        nc.vector.memset(ident[:], 0.0)
+        nc.gpsimd.memset(w_s[:].bitcast(I32), 0)
 
         nc.sync.dma_start(offs_t[:], offs)
-        nc.scalar.dma_start(out=gain[:], in_=gn.rearrange("(p t) o -> p (t o)", t=PACK))
+        nc.scalar.dma_start(out=w_w[:], in_=words_of(w1_words))
+        load_scale_rows([nc.sync, nc.scalar, nc.sync, nc.scalar], x_s, x_scales[0])
+        nc.sync.dma_start(out=x_w[:], in_=words_of(x_words))
+        load_scale_rows([nc.scalar] * 4, w_s, w1_scales[0])
         nc.sync.dma_start(p1_t[:], p1)
         nc.sync.dma_start(p2_t[:], p2)
-        nc.sync.dma_start(out=x_w[:], in_=words_of(x_words))
-        nc.sync.dma_start(out=w_w[:], in_=words_of(w1_words))
-        load_scale_rows([nc.scalar] * 4, x_s, x_scales[0])
-        load_scale_rows([nc.gpsimd, nc.gpsimd, nc.sync, nc.sync], w_s, w1_scales[0])
-        make_identity(nc, ident[:], nomemset=True)
+        nc.sync.dma_start(out=gain[:], in_=gn.rearrange("(p t) o -> p (t o)", t=PACK))
 
         xg_w = keep.tile([P, S], I32, name="xg_w", align_bytes=64)
         xg_s = keep.tile([P, S], U8, name="xg_s", align_bytes=64)
@@ -89,17 +83,14 @@ def tile_picked_zscore3_none_po_kernel(
                 out=dst[:].rearrange("p (t m) -> p t m", t=PACK), in_=src[:].rearrange("p (m t) -> p t m", t=PACK)
             )
 
+        deal(w1d_w, w_w)
         nc.vector.tensor_copy(xg_s[:], x_s[:].indirect(offs_t[:]))
         deal(w1d_s, w_s)
         halves = [slice(0, S // 2), slice(S // 2, S)]
-        w1_view = w_w[:].rearrange("p (m t) -> p t m", t=PACK)
-        nc.vector.tensor_copy(xg_w[:, halves[0]].bitcast(U32), x_w[:].bitcast(U32).indirect(offs_t[:, 0:16]))
-        nc.vector.tensor_copy(out=w1d_w[:, 0:P], in_=w1_view[:, 0, :])
-        nc.vector.tensor_copy(xg_w[:, halves[1]].bitcast(U32), x_w[:].bitcast(U32).indirect(offs_t[:, 16:32]))
-        for t in range(1, PACK):
-            nc.vector.tensor_copy(out=w1d_w[:, t * P : (t + 1) * P], in_=w1_view[:, t, :])
-        nc.vector.tensor_scalar(out=gain_nu[:], in0=gain[:], scalar1=NU, scalar2=None, op0=ALU.mult)
-        nc.vector.tensor_scalar(out=gain_neg[:], in0=gain[:], scalar1=-1.0, scalar2=None, op0=ALU.mult)
+        for half in halves:
+            nc.vector.tensor_copy(
+                xg_w[:, half].bitcast(U32), x_w[:].bitcast(U32).indirect(offs_t[:, half.start // 16 : half.stop // 16])
+            )
 
         y = [keep.tile([P, S], F32, name="y%d" % t) for t in range(PACK)]
         for t in range(PACK):
@@ -113,25 +104,24 @@ def tile_picked_zscore3_none_po_kernel(
                 nc.scalar.copy(out=y[t][:, half], in_=bank[:])
         nc.sync.dma_start(out=w_w[:], in_=words_of(w2_words))
         load_scale_rows([nc.sync] * 4, w_s, w2_scales[0])
-        deal(w2d_w, w_w)
-        deal(w2d_s, w_s)
 
         o_w = keep.tile([P, S], I32, name="o_w", align_bytes=64)
         o_s = keep.tile([P, S], U8, name="o_s", align_bytes=64)
         out_rows = out_0.rearrange("(p t) j -> p t j", t=PACK)
         out_words = words_of(out_1)
-
         state = {}
 
-        def fetch(j0, cw):
+        def fetch(i, j0, cw):
             lst = slice(j0 // 16, (j0 + cw) // 16)
             cols = slice(j0, j0 + cw)
             a = ring.tile([P, PACK, cw], F32, name="a")
             ab = ring.tile([P, PACK, cw], F32, name="ab")
+            d = ring.tile([P, PACK, cw], F32, name="d")
+            w = ring.tile([P, PACK, cw], F32, name="w")
+            n = ring.tile([P, PACK, cw], F32, name="n")
             y_sq = ring.tile([P, PACK, cw], F32, name="y_sq")
-            y_g = ring.tile([P, PACK, cw], F32, name="y_g")
-            for t in range(PACK):
-                nc.scalar.activation(out=y_g[:, t, :], in_=y[t][:, cols], func=ACT.Copy, scale=gain_nu[:, t : t + 1])
+            d_sq = ring.tile([P, PACK, cw], F32, name="d_sq")
+            w_sq = ring.tile([P, PACK, cw], F32, name="w_sq")
             for t in range(PACK):
                 nc.scalar.activation(out=y_sq[:, t, :], in_=y[t][:, cols], func=ACT.Square, scale=math.sqrt(OUTER * PHI))
             for pair in ((0, 1), (2, 3)):
@@ -139,46 +129,42 @@ def tile_picked_zscore3_none_po_kernel(
                     nc.vector.tensor_copy(a[:, t, :], y[t][:].indirect(p1_t[:, lst]))
                 for t in pair:
                     nc.vector.tensor_tensor(ab[:, t, :], y[t][:].indirect(p2_t[:, lst]), a[:, t, :], ALU.add)
-            d = ring.tile([P, PACK, cw], F32, name="d")
-            w = ring.tile([P, PACK, cw], F32, name="w")
-            n = ring.tile([P, PACK, cw], F32, name="n")
             for t in range(PACK):
                 nc.vector.scalar_tensor_tensor(out=w[:, t, :], in0=y[t][:, cols], scalar=ETA, in1=ab[:, t, :], op0=ALU.mult, op1=ALU.subtract)
             nc.vector.scalar_tensor_tensor(out=d[:], in0=a[:], scalar=2.0, in1=ab[:], op0=ALU.mult, op1=ALU.subtract)
             for t in range(PACK):
-                nc.vector.scalar_tensor_tensor(out=n[:, t, :], in0=ab[:, t, :], scalar=gain_neg[:, t : t + 1], in1=y_g[:, t, :], op0=ALU.mult, op1=ALU.add)
-            d_sq = ring.tile([P, PACK, cw], F32, name="d_sq")
-            w_sq = ring.tile([P, PACK, cw], F32, name="w_sq")
+                nc.vector.scalar_tensor_tensor(out=n[:, t, :], in0=y[t][:, cols], scalar=NU, in1=ab[:, t, :], op0=ALU.mult, op1=ALU.subtract)
             nc.scalar.activation(out=w_sq[:], in_=w[:], func=ACT.Square, scale=math.sqrt(OUTER * BETA))
             nc.scalar.activation(out=d_sq[:], in_=d[:], func=ACT.Square, scale=math.sqrt(OUTER * 0.5))
-            state[j0] = (n, [y_sq, w_sq, d_sq])
+            state[i] = (n, y_sq, w_sq, d_sq)
 
-        def spread(j0, cw):
-            n, squares = state[j0]
-            roots = []
-            for b in range(0, cw, BLOCK):
-                var = psum.tile([P, PACK, P], F32, name="bank")
-                for t in range(PACK):
-                    for i, sq in enumerate(squares):
-                        nc.tensor.matmul(var[:, t, :], lhsT=sq[:, t, b : b + BLOCK], rhs=ident[:], is_transpose=True, start=(i == 0), stop=(i == 2))
-                r_turned = ring.tile([P, PACK, P], F32, name="r_turned")
-                nc.scalar.activation(out=r_turned[:], in_=var[:], func=ACT.Abs_reciprocal_sqrt, bias=FLOOR)
-                r = psum.tile([P, PACK, BLOCK], F32, name="bank")
-                for t in range(PACK):
-                    nc.tensor.transpose(r[:, t, :], r_turned[:, t, :], ident[:])
-                roots.append(r)
-            state[j0] = (n, roots)
+        def spread(i, j0, cw):
+            n, y_sq, w_sq, d_sq = state[i]
+            part = ring.tile([P, PACK, cw], F32, name="part")
+            var = ring.tile([P, PACK, cw], F32, name="var")
+            r = ring.tile([P, PACK, cw], F32, name="r")
+            nc.vector.tensor_tensor(part[:], w_sq[:], y_sq[:], ALU.add)
+            nc.vector.tensor_tensor(var[:], part[:], d_sq[:], ALU.add)
+            nc.scalar.activation(out=r[:], in_=var[:], func=ACT.Abs_reciprocal_sqrt, bias=FLOOR)
+            roots = [(0, cw, r)]
+            state[i] = (n, roots)
 
-        def score(j0, cw):
-            n, roots = state[j0]
+        def score(i, j0, cw):
+            n, roots = state[i]
+            z = ring.tile([P, PACK, cw], BF16, name="z", align_bytes=64)
             zi = ring.tile([P, cw, PACK], BF16, name="zi", align_bytes=64)
-            for i, r in enumerate(roots):
-                cols = slice(i * BLOCK, (i + 1) * BLOCK)
-                nc.vector.tensor_tensor(zi[:, cols, :], n[:, :, cols].rearrange("p t j -> p j t"), r[:].rearrange("p t j -> p j t"), ALU.mult)
-            state[j0] = zi
+            for b, bw, r in roots:
+                for t in range(PACK):
+                    nc.vector.scalar_tensor_tensor(out=z[:, t, b : b + bw], in0=n[:, t, b : b + bw], scalar=gain[:, t : t + 1], in1=r[:, t, :], op0=ALU.mult, op1=ALU.mult)
+            weaver = nc.vector.tensor_copy if i == len(CHUNKS) - 1 else nc.scalar.copy
+            weaver(out=zi[:], in_=z[:].rearrange("p t j -> p j t"))
+            state[i] = zi
 
-        def second(j0, cw):
-            zi = state[j0]
+        def second(i, j0, cw):
+            zi = state[i]
+            if i == 0:
+                deal(w2d_w, w_w)
+                deal(w2d_s, w_s)
             z_w = ring.tile([P, cw], U32, name="z_w", align_bytes=64)
             z_s = ring.tile([P, cw], U8, name="z_s", align_bytes=64)
             nc.vector.quantize_mx(out=z_w[:].bitcast(FP8X4), scales=z_s[:], in_=zi[:].rearrange("p j t -> p (j t)"))
@@ -197,10 +183,10 @@ def tile_picked_zscore3_none_po_kernel(
                 nc.scalar.copy(out=o32[:], in_=acc[:])
                 nc.sync.dma_start(out=out_rows[:, :, j0 + b : j0 + b + BLOCK], in_=o32[:])
                 outs.append((j0 + b, o16))
-            state[j0] = outs
+            state[i] = outs
 
-        def planes(j0, cw):
-            for j, o16 in state[j0]:
+        def planes(i, j0, cw):
+            for j, o16 in state[i]:
                 cols = slice(j, j + BLOCK)
                 nc.vector.quantize_mx(out=o_w[:, cols].bitcast(FP8X4), scales=o_s[:, cols], in_=o16[:].rearrange("p j t -> p (j t)"))
             nc.sync.dma_start(out=out_words[:, j0 : j0 + cw], in_=o_w[:, j0 : j0 + cw])
@@ -211,7 +197,7 @@ def tile_picked_zscore3_none_po_kernel(
             for s in reversed(range(len(stages))):
                 i = step - s
                 if 0 <= i < len(CHUNKS):
-                    stages[s](starts[i], CHUNKS[i])
+                    stages[s](i, starts[i], CHUNKS[i])
 
         for q in range(4):
             queue = nc.scalar if q % 2 else nc.sync

@@ -2,6 +2,7 @@ from contextlib import ExitStack
 import math
 
 import concourse.mybir as mybir
+from concourse.masks import make_identity
 
 K, T, S, N, H = 512, 2048, 512, 512, 512
 FLOPS = 2 * K * H * S + 2 * H * N * S
@@ -18,9 +19,12 @@ ACT = mybir.ActivationFunctionType
 
 P = 128
 PACK = 4
+LIST_ROWS = 16
 BLOCK = 128
-CHUNKS = [256,128,128]
-PE_CHUNKS = []
+BLOCKS = S // BLOCK
+LAST = BLOCKS - 1
+WIDE = PACK * BLOCK
+ZEROED_BY_VECTOR = 1600
 
 C = 0.3125
 KAPPA = 2 * C - 3 * C * C
@@ -41,164 +45,198 @@ def words_of(ap):
     return ap[0].rearrange("p n t -> p (n t)").bitcast(I32)
 
 
+def planes_of(ap):
+    return ap.rearrange("p (t j) -> p t j", j=BLOCK)
+
+
+def by_residue(tile):
+    return tile[:].rearrange("p (m t) -> p t m", t=PACK)
+
+
+def interleaved(ap):
+    return ap.rearrange("p t j -> p j t")
+
+
 def tile_picked_zscore3_none_po_kernel(
     tc, x_words, x_scales, w1_words, w1_scales, gn, w2_words, w2_scales, offs, p1, p2, out_0, out_1, out_2
 ):
     nc = tc.nc
     with ExitStack() as ctx:
         keep = ctx.enter_context(tc.tile_pool(name="keep", bufs=1))
-        ring = ctx.enter_context(tc.tile_pool(name="ring", bufs=3))
+        ring = ctx.enter_context(tc.tile_pool(name="ring", bufs=BLOCKS))
         psum = ctx.enter_context(tc.psum_pool(name="psum", bufs=8))
 
-        offs_t = keep.tile([P, S // 16], U16, name="offs_t")
-        p1_t = keep.tile([P, S // 16], U16, name="p1_t")
-        p2_t = keep.tile([P, S // 16], U16, name="p2_t")
+        offs_t = keep.tile([P, S // LIST_ROWS], U16, name="offs_t")
+        p1_t = keep.tile([P, S // LIST_ROWS], U16, name="p1_t")
+        p2_t = keep.tile([P, S // LIST_ROWS], U16, name="p2_t")
         x_w = keep.tile([P, T], I32, name="x_w", align_bytes=64)
         x_s = keep.tile([P, T], U8, name="x_s", align_bytes=64)
-        w_w = keep.tile([P, H], I32, name="w_w", align_bytes=64)
-        w_s = keep.tile([P, H], U8, name="w_s", align_bytes=64)
+        stage_w = keep.tile([P, H], I32, name="stage_w", align_bytes=64)
+        stage_s = keep.tile([P, H], U8, name="stage_s", align_bytes=64)
         gain = keep.tile([P, PACK], F32, name="gain")
+        gain_nu = keep.tile([P, PACK], F32, name="gain_nu")
+        gain_neg = keep.tile([P, PACK], F32, name="gain_neg")
+        ident = keep.tile([P, P], F32, name="ident")
 
-        nc.vector.memset(x_s[:].bitcast(I32), 0)
-        nc.gpsimd.memset(w_s[:].bitcast(I32), 0)
+        nc.vector.memset(x_s[:, 0:ZEROED_BY_VECTOR].bitcast(I32), 0)
+        nc.gpsimd.memset(x_s[:, ZEROED_BY_VECTOR:T].bitcast(I32), 0)
+        nc.vector.memset(stage_s[:].bitcast(I32), 0)
+        make_identity(nc, ident[:])
 
         nc.sync.dma_start(offs_t[:], offs)
-        nc.scalar.dma_start(out=w_w[:], in_=words_of(w1_words))
+        nc.sync.dma_start(out=stage_w[:], in_=words_of(w1_words))
+        nc.sync.dma_start(p1_t[:], p1)
         load_scale_rows([nc.sync, nc.scalar, nc.sync, nc.scalar], x_s, x_scales[0])
         nc.sync.dma_start(out=x_w[:], in_=words_of(x_words))
-        load_scale_rows([nc.scalar] * 4, w_s, w1_scales[0])
-        nc.sync.dma_start(p1_t[:], p1)
+        load_scale_rows([nc.sync] * 4, stage_s, w1_scales[0])
         nc.sync.dma_start(p2_t[:], p2)
         nc.sync.dma_start(out=gain[:], in_=gn.rearrange("(p t) o -> p (t o)", t=PACK))
 
-        xg_w = keep.tile([P, S], I32, name="xg_w", align_bytes=64)
-        xg_s = keep.tile([P, S], U8, name="xg_s", align_bytes=64)
-        w1d_w = keep.tile([P, H], I32, name="w1d_w", align_bytes=64)
-        w1d_s = keep.tile([P, H], U8, name="w1d_s", align_bytes=64)
-        w2d_w = keep.tile([P, N], I32, name="w2d_w", align_bytes=64)
-        w2d_s = keep.tile([P, N], U8, name="w2d_s", align_bytes=64)
+        picked_w = keep.tile([P, S], I32, name="picked_w", align_bytes=64)
+        picked_s = keep.tile([P, S], U8, name="picked_s", align_bytes=64)
+        w1_w = keep.tile([P, H], I32, name="w1_w", align_bytes=64)
+        w1_s = keep.tile([P, H], U8, name="w1_s", align_bytes=64)
+        w2_w = keep.tile([P, N], I32, name="w2_w", align_bytes=64)
+        w2_s = keep.tile([P, N], U8, name="w2_s", align_bytes=64)
 
-        def deal(dst, src):
-            nc.vector.tensor_copy(
-                out=dst[:].rearrange("p (t m) -> p t m", t=PACK), in_=src[:].rearrange("p (m t) -> p t m", t=PACK)
-            )
-
-        deal(w1d_w, w_w)
-        nc.vector.tensor_copy(xg_s[:], x_s[:].indirect(offs_t[:]))
-        deal(w1d_s, w_s)
+        nc.vector.tensor_copy(out=planes_of(w1_w[:]), in_=by_residue(stage_w))
+        nc.vector.tensor_copy(picked_s[:], x_s[:].indirect(offs_t[:]))
+        nc.vector.tensor_copy(out=w1_s[:, 0:P], in_=by_residue(stage_s)[:, 0, :])
         halves = [slice(0, S // 2), slice(S // 2, S)]
         for half in halves:
-            nc.vector.tensor_copy(
-                xg_w[:, half].bitcast(U32), x_w[:].bitcast(U32).indirect(offs_t[:, half.start // 16 : half.stop // 16])
-            )
+            entries = offs_t[:, half.start // LIST_ROWS : half.stop // LIST_ROWS]
+            nc.vector.tensor_copy(picked_w[:, half].bitcast(U32), x_w[:].bitcast(U32).indirect(entries))
+        nc.vector.tensor_copy(out=planes_of(w1_s[:, P:H]), in_=by_residue(stage_s)[:, 1:PACK, :])
 
         y = [keep.tile([P, S], F32, name="y%d" % t) for t in range(PACK)]
         for t in range(PACK):
             cols = slice(t * P, (t + 1) * P)
             for half in halves:
-                bank = psum.tile([P, S // 2], F32, name="bank")
+                y_half = psum.tile([P, S // 2], F32, name="bank")
                 nc.tensor.matmul_mx(
-                    out=bank[:], lhsT=w1d_w[:, cols].bitcast(FP8X4), lhsT_scale=w1d_s[:, cols],
-                    rhs=xg_w[:, half].bitcast(FP8X4), rhs_scale=xg_s[:, half], start=True, stop=True,
+                    out=y_half[:], lhsT=w1_w[:, cols].bitcast(FP8X4), lhsT_scale=w1_s[:, cols],
+                    rhs=picked_w[:, half].bitcast(FP8X4), rhs_scale=picked_s[:, half], start=True, stop=True,
                 )
-                nc.scalar.copy(out=y[t][:, half], in_=bank[:])
-        nc.sync.dma_start(out=w_w[:], in_=words_of(w2_words))
-        load_scale_rows([nc.sync] * 4, w_s, w2_scales[0])
+                nc.scalar.copy(out=y[t][:, half], in_=y_half[:])
 
-        o_w = keep.tile([P, S], I32, name="o_w", align_bytes=64)
-        o_s = keep.tile([P, S], U8, name="o_s", align_bytes=64)
-        out_rows = out_0.rearrange("(p t) j -> p t j", t=PACK)
-        out_words = words_of(out_1)
-        state = {}
+        nc.sync.dma_start(out=stage_w[:], in_=words_of(w2_words))
+        load_scale_rows([nc.sync] * 4, stage_s, w2_scales[0])
 
-        def fetch(i, j0, cw):
-            lst = slice(j0 // 16, (j0 + cw) // 16)
-            cols = slice(j0, j0 + cw)
-            a = ring.tile([P, PACK, cw], F32, name="a")
-            ab = ring.tile([P, PACK, cw], F32, name="ab")
-            d = ring.tile([P, PACK, cw], F32, name="d")
-            w = ring.tile([P, PACK, cw], F32, name="w")
-            n = ring.tile([P, PACK, cw], F32, name="n")
-            y_sq = ring.tile([P, PACK, cw], F32, name="y_sq")
-            d_sq = ring.tile([P, PACK, cw], F32, name="d_sq")
-            w_sq = ring.tile([P, PACK, cw], F32, name="w_sq")
-            for t in range(PACK):
-                nc.scalar.activation(out=y_sq[:, t, :], in_=y[t][:, cols], func=ACT.Square, scale=math.sqrt(OUTER * PHI))
+        y_sq = keep.tile([P, PACK, S], F32, name="y_sq")
+        y_gain = keep.tile([P, PACK, S], F32, name="y_gain")
+        nc.gpsimd.tensor_scalar(out=gain_nu[:], in0=gain[:], scalar1=NU, scalar2=0.0, op0=ALU.mult, op1=ALU.add)
+        nc.gpsimd.tensor_scalar(out=gain_neg[:], in0=gain[:], scalar1=-1.0, scalar2=0.0, op0=ALU.mult, op1=ALU.add)
+        for t in range(PACK):
+            nc.scalar.activation(out=y_sq[:, t, :], in_=y[t][:], func=ACT.Square, scale=math.sqrt(OUTER * PHI))
+        for t in range(PACK):
+            nc.scalar.activation(out=y_gain[:, t, :], in_=y[t][:], func=ACT.Copy, scale=gain_nu[:, t : t + 1])
+
+        sums = []
+        spent = []
+        roots = []
+        scratch = []
+        for i in range(BLOCKS):
+            cols = slice(i * BLOCK, (i + 1) * BLOCK)
+            entries = slice(cols.start // LIST_ROWS, cols.stop // LIST_ROWS)
+            a = ring.tile([P, PACK, BLOCK], F32, name="a")
+            s = ring.tile([P, PACK, BLOCK], F32, name="s")
+            diff = ring.tile([P, PACK, BLOCK], F32, name="diff")
+            lead = ring.tile([P, PACK, BLOCK], F32, name="lead")
+            squares = scratch[i - 2] if i >= 2 else ring.tile([P, 2 * WIDE], F32, name="squares")
+            lead_sq = planes_of(squares[:, 0:WIDE])
+            diff_sq = planes_of(squares[:, WIDE : 2 * WIDE])
+
             for pair in ((0, 1), (2, 3)):
                 for t in pair:
-                    nc.vector.tensor_copy(a[:, t, :], y[t][:].indirect(p1_t[:, lst]))
+                    nc.vector.tensor_copy(a[:, t, :], y[t][:].indirect(p1_t[:, entries]))
                 for t in pair:
-                    nc.vector.tensor_tensor(ab[:, t, :], y[t][:].indirect(p2_t[:, lst]), a[:, t, :], ALU.add)
+                    nc.vector.tensor_tensor(s[:, t, :], y[t][:].indirect(p2_t[:, entries]), a[:, t, :], ALU.add)
             for t in range(PACK):
-                nc.vector.scalar_tensor_tensor(out=w[:, t, :], in0=y[t][:, cols], scalar=ETA, in1=ab[:, t, :], op0=ALU.mult, op1=ALU.subtract)
-            nc.vector.scalar_tensor_tensor(out=d[:], in0=a[:], scalar=2.0, in1=ab[:], op0=ALU.mult, op1=ALU.subtract)
-            for t in range(PACK):
-                nc.vector.scalar_tensor_tensor(out=n[:, t, :], in0=y[t][:, cols], scalar=NU, in1=ab[:, t, :], op0=ALU.mult, op1=ALU.subtract)
-            nc.scalar.activation(out=w_sq[:], in_=w[:], func=ACT.Square, scale=math.sqrt(OUTER * BETA))
-            nc.scalar.activation(out=d_sq[:], in_=d[:], func=ACT.Square, scale=math.sqrt(OUTER * 0.5))
-            state[i] = (n, y_sq, w_sq, d_sq)
+                nc.vector.scalar_tensor_tensor(
+                    out=lead[:, t, :], in0=y[t][:, cols], scalar=ETA, in1=s[:, t, :], op0=ALU.mult, op1=ALU.subtract
+                )
+            nc.vector.scalar_tensor_tensor(out=diff[:], in0=a[:], scalar=2.0, in1=s[:], op0=ALU.mult, op1=ALU.subtract)
+            nc.scalar.activation(out=lead_sq, in_=lead[:], func=ACT.Square, scale=math.sqrt(OUTER * BETA))
+            nc.scalar.activation(out=diff_sq, in_=diff[:], func=ACT.Square, scale=math.sqrt(OUTER * 0.5))
+            sums.append(s)
+            spent.append(diff_sq)
 
-        def spread(i, j0, cw):
-            n, y_sq, w_sq, d_sq = state[i]
-            part = ring.tile([P, PACK, cw], F32, name="part")
-            var = ring.tile([P, PACK, cw], F32, name="var")
-            r = ring.tile([P, PACK, cw], F32, name="r")
-            nc.vector.tensor_tensor(part[:], w_sq[:], y_sq[:], ALU.add)
-            nc.vector.tensor_tensor(var[:], part[:], d_sq[:], ALU.add)
-            nc.scalar.activation(out=r[:], in_=var[:], func=ACT.Abs_reciprocal_sqrt, bias=FLOOR)
-            roots = [(0, cw, r)]
-            state[i] = (n, roots)
-
-        def score(i, j0, cw):
-            n, roots = state[i]
-            z = ring.tile([P, PACK, cw], BF16, name="z", align_bytes=64)
-            zi = ring.tile([P, cw, PACK], BF16, name="zi", align_bytes=64)
-            for b, bw, r in roots:
+            if i < LAST:
+                turned_sum = psum.tile([P, PACK, P], F32, name="bank")
                 for t in range(PACK):
-                    nc.vector.scalar_tensor_tensor(out=z[:, t, b : b + bw], in0=n[:, t, b : b + bw], scalar=gain[:, t : t + 1], in1=r[:, t, :], op0=ALU.mult, op1=ALU.mult)
-            weaver = nc.vector.tensor_copy if i == len(CHUNKS) - 1 else nc.scalar.copy
-            weaver(out=zi[:], in_=z[:].rearrange("p t j -> p j t"))
-            state[i] = zi
+                    terms = (y_sq[:, t, cols], lead_sq[:, t, :], diff_sq[:, t, :])
+                    for k, term in enumerate(terms):
+                        nc.tensor.matmul(
+                            turned_sum[:, t, :], lhsT=term, rhs=ident[:], is_transpose=True,
+                            start=(k == 0), stop=(k == len(terms) - 1),
+                        )
+                own = ring.tile([P, 2 * WIDE], F32, name="scratch")
+                scratch.append(own)
+                turned_root = planes_of(own[:, WIDE // 2 : WIDE // 2 + WIDE])
+                nc.scalar.activation(out=turned_root, in_=turned_sum[:], func=ACT.Abs_reciprocal_sqrt, bias=FLOOR)
+                root = psum.tile([P, PACK, BLOCK], F32, name="bank")
+                for t in range(PACK):
+                    nc.tensor.transpose(root[:, t, :], turned_root[:, t, :], ident[:])
+            else:
+                part = ring.tile([P, PACK, BLOCK], F32, name="part")
+                total = ring.tile([P, PACK, BLOCK], F32, name="total")
+                root = ring.tile([P, PACK, BLOCK], F32, name="root")
+                nc.vector.tensor_tensor(part[:], lead_sq, y_sq[:, :, cols], ALU.add)
+                nc.vector.tensor_tensor(total[:], part[:], diff_sq, ALU.add)
+                nc.scalar.activation(out=root[:], in_=total[:], func=ACT.Abs_reciprocal_sqrt, bias=FLOOR)
+            roots.append(root)
 
-        def second(i, j0, cw):
-            zi = state[i]
+        out_rows = out_0.rearrange("(p t) j -> p t j", t=PACK)
+        rounded = []
+        for i in range(BLOCKS):
+            cols = slice(i * BLOCK, (i + 1) * BLOCK)
+            numerator = spent[i]
+            for t in range(PACK):
+                nc.vector.scalar_tensor_tensor(
+                    out=numerator[:, t, :], in0=sums[i][:, t, :], scalar=gain_neg[:, t : t + 1],
+                    in1=y_gain[:, t, cols], op0=ALU.mult, op1=ALU.add,
+                )
+            z = ring.tile([P, BLOCK, PACK], BF16, name="z", align_bytes=64)
+            if i < LAST:
+                nc.vector.tensor_tensor(z[:], interleaved(numerator), interleaved(roots[i][:]), ALU.mult)
+            else:
+                z_planes = ring.tile([P, PACK, BLOCK], BF16, name="z_planes", align_bytes=64)
+                nc.vector.tensor_tensor(z_planes[:], numerator, roots[i][:], ALU.mult)
+                nc.vector.tensor_copy(out=z[:], in_=interleaved(z_planes[:]))
             if i == 0:
-                deal(w2d_w, w_w)
-                deal(w2d_s, w_s)
-            z_w = ring.tile([P, cw], U32, name="z_w", align_bytes=64)
-            z_s = ring.tile([P, cw], U8, name="z_s", align_bytes=64)
-            nc.vector.quantize_mx(out=z_w[:].bitcast(FP8X4), scales=z_s[:], in_=zi[:].rearrange("p j t -> p (j t)"))
-            outs = []
-            for b in range(0, cw, BLOCK):
-                acc = psum.tile([P, PACK, BLOCK], F32, name="bank")
-                for t in range(PACK):
-                    cols = slice(t * P, (t + 1) * P)
-                    nc.tensor.matmul_mx(
-                        out=acc[:, t, :], lhsT=w2d_w[:, cols].bitcast(FP8X4), lhsT_scale=w2d_s[:, cols],
-                        rhs=z_w[:, b : b + BLOCK].bitcast(FP8X4), rhs_scale=z_s[:, b : b + BLOCK], start=True, stop=True,
-                    )
-                o32 = keep.tile([P, PACK, BLOCK], F32, name="o32_%d" % (j0 + b))
-                o16 = keep.tile([P, BLOCK, PACK], BF16, name="o16_%d" % (j0 + b), align_bytes=64)
-                nc.scalar.copy(out=o16[:], in_=acc[:].rearrange("p t j -> p j t"))
-                nc.scalar.copy(out=o32[:], in_=acc[:])
-                nc.sync.dma_start(out=out_rows[:, :, j0 + b : j0 + b + BLOCK], in_=o32[:])
-                outs.append((j0 + b, o16))
-            state[i] = outs
+                nc.vector.tensor_copy(out=planes_of(w2_w[:]), in_=by_residue(stage_w))
+                nc.vector.tensor_copy(out=planes_of(w2_s[:]), in_=by_residue(stage_s))
+            z_w = ring.tile([P, BLOCK], U32, name="z_w", align_bytes=64)
+            z_s = ring.tile([P, BLOCK], U8, name="z_s", align_bytes=64)
+            nc.vector.quantize_mx(out=z_w[:].bitcast(FP8X4), scales=z_s[:], in_=z[:].rearrange("p j t -> p (j t)"))
 
-        def planes(i, j0, cw):
-            for j, o16 in state[i]:
-                cols = slice(j, j + BLOCK)
-                nc.vector.quantize_mx(out=o_w[:, cols].bitcast(FP8X4), scales=o_s[:, cols], in_=o16[:].rearrange("p j t -> p (j t)"))
-            nc.sync.dma_start(out=out_words[:, j0 : j0 + cw], in_=o_w[:, j0 : j0 + cw])
+            result = psum.tile([P, PACK, BLOCK], F32, name="bank")
+            for t in range(PACK):
+                rows = slice(t * P, (t + 1) * P)
+                nc.tensor.matmul_mx(
+                    out=result[:, t, :], lhsT=w2_w[:, rows].bitcast(FP8X4), lhsT_scale=w2_s[:, rows],
+                    rhs=z_w[:].bitcast(FP8X4), rhs_scale=z_s[:], start=True, stop=True,
+                )
+            out_f32 = ring.tile([P, PACK, BLOCK], F32, name="out_f32")
+            out_bf16 = ring.tile([P, BLOCK, PACK], BF16, name="out_bf16", align_bytes=64)
+            if i < LAST:
+                nc.scalar.copy(out=out_bf16[:], in_=interleaved(result[:]))
+            else:
+                nc.vector.tensor_copy(out=out_bf16[:], in_=interleaved(result[:]))
+            nc.scalar.copy(out=out_f32[:], in_=result[:])
+            nc.sync.dma_start(out=out_rows[:, :, cols], in_=out_f32[:])
+            rounded.append(out_bf16)
 
-        starts = [sum(CHUNKS[:i]) for i in range(len(CHUNKS))]
-        stages = [fetch, spread, score, second, planes]
-        for step in range(len(CHUNKS) + len(stages) - 1):
-            for s in reversed(range(len(stages))):
-                i = step - s
-                if 0 <= i < len(CHUNKS):
-                    stages[s](i, starts[i], CHUNKS[i])
-
+        out_w = keep.tile([P, S], I32, name="out_w", align_bytes=64)
+        out_s = keep.tile([P, S], U8, name="out_s", align_bytes=64)
+        for i in range(BLOCKS):
+            cols = slice(i * BLOCK, (i + 1) * BLOCK)
+            nc.vector.quantize_mx(
+                out=out_w[:, cols].bitcast(FP8X4), scales=out_s[:, cols], in_=rounded[i][:].rearrange("p j t -> p (j t)")
+            )
+            nc.sync.dma_start(out=words_of(out_1)[:, cols], in_=out_w[:, cols])
         for q in range(4):
             queue = nc.scalar if q % 2 else nc.sync
-            queue.dma_start(out=out_2[0][4 * q : 4 * q + 4, :].bitcast(I32), in_=o_s[32 * q : 32 * q + 4, :].bitcast(I32))
+            queue.dma_start(
+                out=out_2[0][4 * q : 4 * q + 4, :].bitcast(I32), in_=out_s[32 * q : 32 * q + 4, :].bitcast(I32)
+            )

@@ -23,6 +23,7 @@ LIST_ROWS = 16
 BLOCK = 128
 BLOCKS = S // BLOCK
 LAST = BLOCKS - 1
+W2_ROWS = 4
 WIDE = PACK * BLOCK
 ZEROED_BY_VECTOR = 1600
 
@@ -36,9 +37,10 @@ OUTER = 0.25 / (C * C)
 FLOOR = 0.1 / (C * C)
 
 
-def load_scale_rows(queues, tile, rows):
+def load_scale_rows(queues, tile, rows, first=0):
     for q in range(4):
-        queues[q].dma_start(out=tile[32 * q : 32 * q + 4, :].bitcast(I32), in_=rows[4 * q : 4 * q + 4, :].bitcast(I32))
+        to = 32 * q + first
+        queues[q].dma_start(out=tile[to : to + 4, :].bitcast(I32), in_=rows[4 * q : 4 * q + 4, :].bitcast(I32))
 
 
 def words_of(ap):
@@ -89,24 +91,24 @@ def tile_picked_zscore3_none_po_kernel(
         load_scale_rows([nc.sync, nc.scalar, nc.sync, nc.scalar], x_s, x_scales[0])
         nc.sync.dma_start(out=x_w[:], in_=words_of(x_words))
         load_scale_rows([nc.sync] * 4, stage_s, w1_scales[0])
+        load_scale_rows([nc.gpsimd] + [nc.sync] * 3, stage_s, w2_scales[0], first=W2_ROWS)
         nc.sync.dma_start(p2_t[:], p2)
         nc.sync.dma_start(out=gain[:], in_=gn.rearrange("(p t) o -> p (t o)", t=PACK))
 
         picked_w = keep.tile([P, S], I32, name="picked_w", align_bytes=64)
         picked_s = keep.tile([P, S], U8, name="picked_s", align_bytes=64)
         w1_w = keep.tile([P, H], I32, name="w1_w", align_bytes=64)
-        w1_s = keep.tile([P, H], U8, name="w1_s", align_bytes=64)
+        w_s = keep.tile([P, H], U8, name="w_s", align_bytes=64)
         w2_w = keep.tile([P, N], I32, name="w2_w", align_bytes=64)
-        w2_s = keep.tile([P, N], U8, name="w2_s", align_bytes=64)
 
         nc.vector.tensor_copy(out=planes_of(w1_w[:]), in_=by_residue(stage_w))
         nc.vector.tensor_copy(picked_s[:], x_s[:].indirect(offs_t[:]))
-        nc.vector.tensor_copy(out=w1_s[:, 0:P], in_=by_residue(stage_s)[:, 0, :])
+        nc.vector.tensor_copy(out=w_s[:, 0:P], in_=by_residue(stage_s)[:, 0, :])
         halves = [slice(0, S // 2), slice(S // 2, S)]
         for half in halves:
             entries = offs_t[:, half.start // LIST_ROWS : half.stop // LIST_ROWS]
             nc.vector.tensor_copy(picked_w[:, half].bitcast(U32), x_w[:].bitcast(U32).indirect(entries))
-        nc.vector.tensor_copy(out=planes_of(w1_s[:, P:H]), in_=by_residue(stage_s)[:, 1:PACK, :])
+        nc.vector.tensor_copy(out=planes_of(w_s[:, P:H]), in_=by_residue(stage_s)[:, 1:PACK, :])
 
         y = [keep.tile([P, S], F32, name="y%d" % t) for t in range(PACK)]
         for t in range(PACK):
@@ -114,13 +116,12 @@ def tile_picked_zscore3_none_po_kernel(
             for half in halves:
                 y_half = psum.tile([P, S // 2], F32, name="bank")
                 nc.tensor.matmul_mx(
-                    out=y_half[:], lhsT=w1_w[:, cols].bitcast(FP8X4), lhsT_scale=w1_s[:, cols],
+                    out=y_half[:], lhsT=w1_w[:, cols].bitcast(FP8X4), lhsT_scale=w_s[:, cols],
                     rhs=picked_w[:, half].bitcast(FP8X4), rhs_scale=picked_s[:, half], start=True, stop=True,
                 )
                 nc.scalar.copy(out=y[t][:, half], in_=y_half[:])
 
         nc.sync.dma_start(out=stage_w[:], in_=words_of(w2_words))
-        load_scale_rows([nc.sync] * 4, stage_s, w2_scales[0])
 
         y_sq = keep.tile([P, PACK, S], F32, name="y_sq")
         y_gain = keep.tile([P, PACK, S], F32, name="y_gain")
@@ -177,14 +178,15 @@ def tile_picked_zscore3_none_po_kernel(
                 root = psum.tile([P, PACK, BLOCK], F32, name="bank")
                 for t in range(PACK):
                     nc.tensor.transpose(root[:, t, :], turned_root[:, t, :], ident[:])
+                roots.append(interleaved(root[:]))
             else:
                 part = ring.tile([P, PACK, BLOCK], F32, name="part")
                 total = ring.tile([P, PACK, BLOCK], F32, name="total")
-                root = ring.tile([P, PACK, BLOCK], F32, name="root")
+                root_tile = ring.tile([P, BLOCK, PACK], F32, name="root_tile")
                 nc.vector.tensor_tensor(part[:], lead_sq, y_sq[:, :, cols], ALU.add)
                 nc.vector.tensor_tensor(total[:], part[:], diff_sq, ALU.add)
-                nc.scalar.activation(out=root[:], in_=total[:], func=ACT.Abs_reciprocal_sqrt, bias=FLOOR)
-            roots.append(root)
+                nc.scalar.activation(out=root_tile[:], in_=interleaved(total[:]), func=ACT.Abs_reciprocal_sqrt, bias=FLOOR)
+                roots.append(root_tile[:])
 
         out_rows = out_0.rearrange("(p t) j -> p t j", t=PACK)
         rounded = []
@@ -197,15 +199,9 @@ def tile_picked_zscore3_none_po_kernel(
                     in1=y_gain[:, t, cols], op0=ALU.mult, op1=ALU.add,
                 )
             z = ring.tile([P, BLOCK, PACK], BF16, name="z", align_bytes=64)
-            if i < LAST:
-                nc.vector.tensor_tensor(z[:], interleaved(numerator), interleaved(roots[i][:]), ALU.mult)
-            else:
-                z_planes = ring.tile([P, PACK, BLOCK], BF16, name="z_planes", align_bytes=64)
-                nc.vector.tensor_tensor(z_planes[:], numerator, roots[i][:], ALU.mult)
-                nc.vector.tensor_copy(out=z[:], in_=interleaved(z_planes[:]))
+            nc.vector.tensor_tensor(z[:], interleaved(numerator), roots[i], ALU.mult)
             if i == 0:
                 nc.vector.tensor_copy(out=planes_of(w2_w[:]), in_=by_residue(stage_w))
-                nc.vector.tensor_copy(out=planes_of(w2_s[:]), in_=by_residue(stage_s))
             z_w = ring.tile([P, BLOCK], U32, name="z_w", align_bytes=64)
             z_s = ring.tile([P, BLOCK], U8, name="z_s", align_bytes=64)
             nc.vector.quantize_mx(out=z_w[:].bitcast(FP8X4), scales=z_s[:], in_=z[:].rearrange("p j t -> p (j t)"))
@@ -214,7 +210,7 @@ def tile_picked_zscore3_none_po_kernel(
             for t in range(PACK):
                 rows = slice(t * P, (t + 1) * P)
                 nc.tensor.matmul_mx(
-                    out=result[:, t, :], lhsT=w2_w[:, rows].bitcast(FP8X4), lhsT_scale=w2_s[:, rows],
+                    out=result[:, t, :], lhsT=w2_w[:, rows].bitcast(FP8X4), lhsT_scale=w_s[W2_ROWS:P, rows],
                     rhs=z_w[:].bitcast(FP8X4), rhs_scale=z_s[:], start=True, stop=True,
                 )
             out_f32 = ring.tile([P, PACK, BLOCK], F32, name="out_f32")

from contextlib import ExitStack
import math

import concourse.mybir as mybir
from concourse.masks import make_identity

K, T, S, N, H = 512, 2048, 512, 512, 512
FLOPS = 2 * K * H * S + 2 * H * N * S

F32 = mybir.dt.float32
BF16 = mybir.dt.bfloat16
I32 = mybir.dt.int32
U32 = mybir.dt.uint32
U16 = mybir.dt.uint16
U8 = mybir.dt.uint8
FP8X4 = mybir.dt.float8_e4m3fn_x4
ALU = mybir.AluOpType
ACT = mybir.ActivationFunctionType

P = 128
PACK = 4
LIST_ROWS = 16
BLOCK = 128
BLOCKS = S // BLOCK
LAST = BLOCKS - 1
W2_ROWS = 4
WIDE = PACK * BLOCK
ZEROED_BY_VECTOR = 1600

C = 0.3125
KAPPA = 2 * C - 3 * C * C
BETA = 0.5 - KAPPA
ETA = KAPPA / BETA
PHI = 1.0 - KAPPA - KAPPA * KAPPA / BETA
NU = (1.0 - C) / C
OUTER = 0.25 / (C * C)
FLOOR = 0.1 / (C * C)


def load_scale_rows(queues, tile, rows, first=0):
    for q in range(4):
        to = 32 * q + first
        queues[q].dma_start(out=tile[to : to + 4, :].bitcast(I32), in_=rows[4 * q : 4 * q + 4, :].bitcast(I32))


def words_of(ap):
    return ap[0].rearrange("p n t -> p (n t)").bitcast(I32)


def planes_of(ap):
    return ap.rearrange("p (t j) -> p t j", j=BLOCK)


def by_residue(tile):
    return tile[:].rearrange("p (m t) -> p t m", t=PACK)


def interleaved(ap):
    return ap.rearrange("p t j -> p j t")


def tile_picked_zscore3_none_po_kernel(
    tc, x_words, x_scales, w1_words, w1_scales, gn, w2_words, w2_scales, offs, p1, p2, out_0, out_1, out_2
):
    nc = tc.nc
    with ExitStack() as ctx:
        keep = ctx.enter_context(tc.tile_pool(name="keep", bufs=1))
        ring = ctx.enter_context(tc.tile_pool(name="ring", bufs=BLOCKS))
        psum = ctx.enter_context(tc.psum_pool(name="psum", bufs=8))

        offs_t = keep.tile([P, S // LIST_ROWS], U16, name="offs_t")
        p1_t = keep.tile([P, S // LIST_ROWS], U16, name="p1_t")
        p2_t = keep.tile([P, S // LIST_ROWS], U16, name="p2_t")
        x_w = keep.tile([P, T], I32, name="x_w", align_bytes=64)
        x_s = keep.tile([P, T], U8, name="x_s", align_bytes=64)
        stage_w = keep.tile([P, H], I32, name="stage_w", align_bytes=64)
        stage_s = keep.tile([P, H], U8, name="stage_s", align_bytes=64)
        gain = keep.tile([P, PACK], F32, name="gain")
        gain_nu = keep.tile([P, PACK], F32, name="gain_nu")
        gain_neg = keep.tile([P, PACK], F32, name="gain_neg")
        ident = keep.tile([P, P], F32, name="ident")

        nc.vector.memset(x_s[:, 0:ZEROED_BY_VECTOR].bitcast(I32), 0)
        nc.gpsimd.memset(x_s[:, ZEROED_BY_VECTOR:T].bitcast(I32), 0)
        nc.vector.memset(stage_s[:].bitcast(I32), 0)
        make_identity(nc, ident[:])

        nc.sync.dma_start(offs_t[:], offs)
        nc.sync.dma_start(out=stage_w[:], in_=words_of(w1_words))
        nc.sync.dma_start(p1_t[:], p1)
        load_scale_rows([nc.sync, nc.scalar, nc.sync, nc.scalar], x_s, x_scales[0])
        nc.sync.dma_start(out=x_w[:], in_=words_of(x_words))
        load_scale_rows([nc.sync] * 4, stage_s, w1_scales[0])
        load_scale_rows([nc.gpsimd] + [nc.sync] * 3, stage_s, w2_scales[0], first=W2_ROWS)
        nc.sync.dma_start(p2_t[:], p2)
        nc.sync.dma_start(out=gain[:], in_=gn.rearrange("(p t) o -> p (t o)", t=PACK))

        picked_w = keep.tile([P, S], I32, name="picked_w", align_bytes=64)
        picked_s = keep.tile([P, S], U8, name="picked_s", align_bytes=64)
        w1_w = keep.tile([P, H], I32, name="w1_w", align_bytes=64)
        w_s = keep.tile([P, H], U8, name="w_s", align_bytes=64)
        w2_w = keep.tile([P, N], I32, name="w2_w", align_bytes=64)

        nc.vector.tensor_copy(out=planes_of(w1_w[:]), in_=by_residue(stage_w))
        nc.vector.tensor_copy(picked_s[:], x_s[:].indirect(offs_t[:]))
        nc.vector.tensor_copy(out=w_s[:, 0:P], in_=by_residue(stage_s)[:, 0, :])
        halves = [slice(0, S // 2), slice(S // 2, S)]
        for half in halves:
            entries = offs_t[:, half.start // LIST_ROWS : half.stop // LIST_ROWS]
            nc.vector.tensor_copy(picked_w[:, half].bitcast(U32), x_w[:].bitcast(U32).indirect(entries))
        nc.vector.tensor_copy(out=planes_of(w_s[:, P:H]), in_=by_residue(stage_s)[:, 1:PACK, :])

        y = [keep.tile([P, S], F32, name="y%d" % t) for t in range(PACK)]
        for t in range(PACK):
            cols = slice(t * P, (t + 1) * P)
            for half in halves:
                y_half = psum.tile([P, S // 2], F32, name="bank")
                nc.tensor.matmul_mx(
                    out=y_half[:], lhsT=w1_w[:, cols].bitcast(FP8X4), lhsT_scale=w_s[:, cols],
                    rhs=picked_w[:, half].bitcast(FP8X4), rhs_scale=picked_s[:, half], start=True, stop=True,
                )
                nc.scalar.copy(out=y[t][:, half], in_=y_half[:])

        nc.sync.dma_start(out=stage_w[:], in_=words_of(w2_words))

        y_sq = keep.tile([P, PACK, S], F32, name="y_sq")
        y_gain = keep.tile([P, PACK, S], F32, name="y_gain")
        nc.gpsimd.tensor_scalar(out=gain_nu[:], in0=gain[:], scalar1=NU, scalar2=0.0, op0=ALU.mult, op1=ALU.add)
        nc.gpsimd.tensor_scalar(out=gain_neg[:], in0=gain[:], scalar1=-1.0, scalar2=0.0, op0=ALU.mult, op1=ALU.add)
        for t in range(PACK):
            nc.scalar.activation(out=y_sq[:, t, :], in_=y[t][:], func=ACT.Square, scale=math.sqrt(OUTER * PHI))
        for t in range(PACK):
            nc.scalar.activation(out=y_gain[:, t, :], in_=y[t][:], func=ACT.Copy, scale=gain_nu[:, t : t + 1])

        sums = []
        spent = []
        roots = []
        scratch = []
        for i in range(BLOCKS):
            cols = slice(i * BLOCK, (i + 1) * BLOCK)
            entries = slice(cols.start // LIST_ROWS, cols.stop // LIST_ROWS)
            a = ring.tile([P, PACK, BLOCK], F32, name="a")
            s = ring.tile([P, PACK, BLOCK], F32, name="s")
            diff = ring.tile([P, PACK, BLOCK], F32, name="diff")
            lead = ring.tile([P, PACK, BLOCK], F32, name="lead")
            squares = scratch[i - 2] if i >= 2 else ring.tile([P, 2 * WIDE], F32, name="squares")
            lead_sq = planes_of(squares[:, 0:WIDE])
            diff_sq = planes_of(squares[:, WIDE : 2 * WIDE])

            for pair in ((0, 1), (2, 3)):
                for t in pair:
                    nc.vector.tensor_copy(a[:, t, :], y[t][:].indirect(p1_t[:, entries]))
                for t in pair:
                    nc.vector.tensor_tensor(s[:, t, :], y[t][:].indirect(p2_t[:, entries]), a[:, t, :], ALU.add)
            for t in range(PACK):
                nc.vector.scalar_tensor_tensor(
                    out=lead[:, t, :], in0=y[t][:, cols], scalar=ETA, in1=s[:, t, :], op0=ALU.mult, op1=ALU.subtract
                )
            nc.vector.scalar_tensor_tensor(out=diff[:], in0=a[:], scalar=2.0, in1=s[:], op0=ALU.mult, op1=ALU.subtract)
            nc.scalar.activation(out=lead_sq, in_=lead[:], func=ACT.Square, scale=math.sqrt(OUTER * BETA))
            nc.scalar.activation(out=diff_sq, in_=diff[:], func=ACT.Square, scale=math.sqrt(OUTER * 0.5))
            sums.append(s)
            spent.append(diff_sq)

            if i < LAST:
                turned_sum = psum.tile([P, PACK, P], F32, name="bank")
                for t in range(PACK):
                    terms = (y_sq[:, t, cols], lead_sq[:, t, :], diff_sq[:, t, :])
                    for k, term in enumerate(terms):
                        nc.tensor.matmul(
                            turned_sum[:, t, :], lhsT=term, rhs=ident[:], is_transpose=True,
                            start=(k == 0), stop=(k == len(terms) - 1),
                        )
                own = ring.tile([P, 2 * WIDE], F32, name="scratch")
                scratch.append(own)
                turned_root = planes_of(own[:, WIDE // 2 : WIDE // 2 + WIDE])
                nc.scalar.activation(out=turned_root, in_=turned_sum[:], func=ACT.Abs_reciprocal_sqrt, bias=FLOOR)
                root = psum.tile([P, PACK, BLOCK], F32, name="bank")
                for t in range(PACK):
                    nc.tensor.transpose(root[:, t, :], turned_root[:, t, :], ident[:])
                roots.append(interleaved(root[:]))
            else:
                part = ring.tile([P, PACK, BLOCK], F32, name="part")
                total = ring.tile([P, PACK, BLOCK], F32, name="total")
                root_tile = ring.tile([P, BLOCK, PACK], F32, name="root_tile")
                nc.vector.tensor_tensor(part[:], lead_sq, y_sq[:, :, cols], ALU.add)
                nc.vector.tensor_tensor(total[:], part[:], diff_sq, ALU.add)
                nc.scalar.activation(out=root_tile[:], in_=interleaved(total[:]), func=ACT.Abs_reciprocal_sqrt, bias=FLOOR)
                roots.append(root_tile[:])

        out_rows = out_0.rearrange("(p t) j -> p t j", t=PACK)
        rounded = []
        for i in range(BLOCKS):
            cols = slice(i * BLOCK, (i + 1) * BLOCK)
            numerator = spent[i]
            for t in range(PACK):
                nc.vector.scalar_tensor_tensor(
                    out=numerator[:, t, :], in0=sums[i][:, t, :], scalar=gain_neg[:, t : t + 1],
                    in1=y_gain[:, t, cols], op0=ALU.mult, op1=ALU.add,
                )
            z = ring.tile([P, BLOCK, PACK], BF16, name="z", align_bytes=64)
            nc.vector.tensor_tensor(z[:], interleaved(numerator), roots[i], ALU.mult)
            if i == 0:
                nc.vector.tensor_copy(out=planes_of(w2_w[:]), in_=by_residue(stage_w))
            z_w = ring.tile([P, BLOCK], U32, name="z_w", align_bytes=64)
            z_s = ring.tile([P, BLOCK], U8, name="z_s", align_bytes=64)
            nc.vector.quantize_mx(out=z_w[:].bitcast(FP8X4), scales=z_s[:], in_=z[:].rearrange("p j t -> p (j t)"))

            result = psum.tile([P, PACK, BLOCK], F32, name="bank")
            for t in range(PACK):
                rows = slice(t * P, (t + 1) * P)
                nc.tensor.matmul_mx(
                    out=result[:, t, :], lhsT=w2_w[:, rows].bitcast(FP8X4), lhsT_scale=w_s[W2_ROWS:P, rows],
                    rhs=z_w[:].bitcast(FP8X4), rhs_scale=z_s[:], start=True, stop=True,
                )
            out_f32 = ring.tile([P, PACK, BLOCK], F32, name="out_f32")
            out_bf16 = ring.tile([P, BLOCK, PACK], BF16, name="out_bf16", align_bytes=64)
            if i < LAST:
                nc.scalar.copy(out=out_bf16[:], in_=interleaved(result[:]))
            else:
                nc.vector.tensor_copy(out=out_bf16[:], in_=interleaved(result[:]))
            nc.scalar.copy(out=out_f32[:], in_=result[:])
            nc.sync.dma_start(out=out_rows[:, :, cols], in_=out_f32[:])
            rounded.append(out_bf16)

        out_w = keep.tile([P, S], I32, name="out_w", align_bytes=64)
        out_s = keep.tile([P, S], U8, name="out_s", align_bytes=64)
        for i in range(BLOCKS):
            cols = slice(i * BLOCK, (i + 1) * BLOCK)
            nc.vector.quantize_mx(
                out=out_w[:, cols].bitcast(FP8X4), scales=out_s[:, cols], in_=rounded[i][:].rearrange("p j t -> p (j t)")
            )
            nc.sync.dma_start(out=words_of(out_1)[:, cols], in_=out_w[:, cols])
        for q in range(4):
            queue = nc.scalar if q % 2 else nc.sync
            queue.dma_start(
                out=out_2[0][4 * q : 4 * q + 4, :].bitcast(I32), in_=out_s[32 * q : 32 * q + 4, :].bitcast(I32)
            )
